import numpy as np
import ml_dtypes


def mxq(x, axis, fmt="e4m3"):
    dtype, down = {"e4m3": (ml_dtypes.float8_e4m3fn, 7), "e5m2": (ml_dtypes.float8_e5m2, 14)}[fmt]
    v = np.moveaxis(np.asarray(x, np.float32).astype(ml_dtypes.bfloat16).astype(np.float64), axis, -1)
    blocks = v.reshape(v.shape[:-1] + (-1, 32))
    amax = np.abs(blocks).max(-1, keepdims=True)
    byte = np.maximum(np.where(amax > 0, np.frexp(amax)[1] - 1 + 127, 0) - down, 1)
    scale = np.exp2(byte - 127.0)
    codes = (blocks / scale).astype(np.float32).astype(dtype).astype(np.float64)
    return np.moveaxis((codes * scale).reshape(v.shape), -1, axis)


WIDE = False


def mx_kscale(k):
    if not WIDE:
        return np.ones(k)
    levels = np.array([30, -30])
    if k % 512:
        return np.exp2(np.random.permutation(np.resize(levels, k // 32))).repeat(32)
    a = np.empty((k // 512, 16))
    for p in range(k // 512):
        a[p, :8] = np.random.permutation(np.resize(levels, 8))
        for g in range(8):
            far = levels[np.abs(levels - a[p, g]) >= 10]
            a[p, g + 8] = far[np.random.randint(len(far))]
    return np.exp2(a.ravel()).repeat(32)


def f64(x):
    return np.asarray(x).astype(np.float64)


def striped(idx):
    return np.tile(np.asarray(idx).reshape(-1, 16).T, (8, 1)).astype(np.uint16)


def unstriped(offs):
    return offs[:16].T.reshape(-1).astype(np.int64)


E2M1 = np.array([0.0, 0.5, 1.0, 1.5, 2.0, 3.0, 4.0, 6.0, -0.0, -0.5, -1.0, -1.5, -2.0, -3.0, -4.0, -6.0])


def pack_weight(w, fmt):
    k, n = w.shape
    w = f64(np.asarray(w, np.float32).astype(ml_dtypes.bfloat16)).reshape(k // 32, 32, n)
    amax = np.abs(w).max(1)
    if fmt in ("e4m3", "e5m2"):
        byte = np.frexp(amax)[1] - 1 + 127 - (7 if fmt == "e4m3" else 14)
    else:
        mant, ex = np.frexp(amax / 6.0)
        byte = np.where(mant > 0.5, ex, ex - 1) + 127
    byte = np.clip(np.where(amax > 0, byte, 1), 1, 254)
    scaled = (w * np.exp2(127.0 - byte)[:, None, :]).reshape(k, n).astype(np.float32)
    by_word = np.ascontiguousarray(scaled.reshape(k // 512, 128, 4, n).transpose(0, 1, 3, 2))
    if fmt in ("e4m3", "e5m2"):
        words = by_word.astype(ml_dtypes.float8_e4m3fn if fmt == "e4m3" else ml_dtypes.float8_e5m2).view(np.uint8)
    else:
        c = by_word.astype(ml_dtypes.float4_e2m1fn).view(np.uint8) & 0xF
        words = (c[..., 0::2] | (c[..., 1::2] << 4)).reshape(k // 512, 128, 2 * n)
    return np.ascontiguousarray(words), np.ascontiguousarray(byte.astype(np.uint8).reshape(k // 512, 16, n))


def unpack_weight(words, scales, fmt):
    g, _, n = scales.shape
    words = np.ascontiguousarray(words).reshape(g, 128, n, -1)
    if fmt in ("e4m3", "e5m2"):
        vals = words.view(ml_dtypes.float8_e4m3fn if fmt == "e4m3" else ml_dtypes.float8_e5m2).astype(np.float64)
    else:
        nib = np.empty((g, 128, n, 4), np.uint8)
        nib[..., 0::2] = words & 0xF
        nib[..., 1::2] = words >> 4
        vals = E2M1[nib]
    vals = vals * np.repeat(np.exp2(scales.astype(np.float64) - 127.0), 8, axis=1)[..., None]
    return vals.transpose(0, 1, 3, 2).reshape(g * 512, n)


K, T, J, I, S, G = 1024, 1024, 256, 256, 512, 32


def setup_inputs():
    n = np.random.standard_normal
    idx = np.random.permutation(T)[:J]
    idx2 = np.random.permutation(S)[:J]
    fk = mx_kscale(K)
    kyp = pack_weight(n((K, I)) / fk[:, None], "e5m2")
    return {
        "xf": (n((K, T)) * 0.03).astype(np.float32),
        "xb": (n((K, S))).astype(np.float32),
        "fk": (np.random.uniform(0.5, 2.0, (K, 1)) * fk[:, None]).astype(np.float32),
        "ky_words": kyp[0],
        "ky_scales": kyp[1],
        "bi": (np.random.uniform(-0.7, 0.7, (1, I))).astype(np.float32),
        "offs": striped(idx),
        "offs2": striped(idx2),
    }


def reference(xf, xb, fk, ky_words, ky_scales, bi, offs, offs2):
    idx = unstriped(offs)
    idx2 = unstriped(offs2)
    kyu = unpack_weight(ky_words, ky_scales, "e5m2")
    u = f64(xf)[:, idx] * f64(xb)[:, idx2] * f64(fk)
    uq = mxq(u, 0, "e5m2")
    a0 = uq.T @ kyu
    a = a0 + f64(bi)
    g1 = a.reshape(J, G, I // G).mean(axis=2)
    g2 = np.repeat(g1, I // G, axis=1)
    y = (a - g2) * np.abs(a)
    return y

@@ -1,0 +1,165 @@
+from contextlib import ExitStack
+
+import concourse.mybir as mybir
+from concourse.masks import make_identity
+
+K, T, J, I, S, BUNDLE = 1024, 1024, 256, 256, 512, 8
+FLOPS = 2 * K * J * I
+
+F32 = mybir.dt.float32
+BF16 = mybir.dt.bfloat16
+I32 = mybir.dt.int32
+U32 = mybir.dt.uint32
+U16 = mybir.dt.uint16
+U8 = mybir.dt.uint8
+E5M2X4 = mybir.dt.float8_e5m2_x4
+ALU = mybir.AluOpType
+ACT = mybir.ActivationFunctionType
+
+P = 128
+PACK = 4
+K_PASS = P * PACK
+PASSES = K // K_PASS
+HALVES = J // P
+LIST_COLS = P // 16
+
+
+def tile_list_scores_products_given_centred_kernel(tc, xf, xb, fk, ky_words, ky_scales, bi, offs, offs2, out):
+    nc = tc.nc
+    with ExitStack() as ctx:
+        keep = ctx.enter_context(tc.tile_pool(name="keep", bufs=1))
+        psum = ctx.enter_context(tc.psum_pool(name="psum", bufs=1))
+
+        tok_list = keep.tile([P, J // 16], U16, name="tok_list")
+        ent_list = keep.tile([P, J // 16], U16, name="ent_list")
+        xb_sb = [keep.tile([P, PACK * S], F32, name=f"xb_{z}") for z in range(PASSES)]
+        xf_sb = [[keep.tile([P, T], F32, name=f"xf_{z}_{t}") for t in range(PACK)] for z in range(PASSES)]
+        fk_sb = keep.tile([P, PASSES, 2 * PACK], F32, name="fk_sb")
+        bi_col = keep.tile([P, 2], F32, name="bi_col")
+        key_words = keep.tile([P, PASSES, I], U32, name="key_words", align_bytes=64)
+        key_scales = keep.tile([P, PASSES * I], U8, name="key_scales", align_bytes=64)
+
+        def load_xb(z):
+            rows = xb[z * K_PASS : (z + 1) * K_PASS, :]
+            nc.sync.dma_start(xb_sb[z][:], rows.rearrange("(p t) s -> p (t s)", t=PACK))
+
+        def load_xf(z, t):
+            rows = xf[z * K_PASS : (z + 1) * K_PASS, :]
+            nc.sync.dma_start(xf_sb[z][t][:], rows.rearrange("(p t) c -> p t c", t=PACK)[:, t, :])
+
+        load_xb(0)
+        nc.sync.dma_start(ent_list[:], offs2)
+        nc.sync.dma_start(tok_list[:], offs)
+        load_xb(1)
+        nc.sync.dma_start(bi_col[:], bi.rearrange("o (p c) -> p (o c)", c=2))
+        nc.sync.dma_start(fk_sb[:, :, 0:PACK], fk.rearrange("(z p t) o -> p z (t o)", z=PASSES, t=PACK))
+        for z in range(PASSES):
+            for t in range(PACK):
+                load_xf(z, t)
+        nc.sync.dma_start(key_words[:].bitcast(I32), ky_words.rearrange("z p c r -> p z (c r)").bitcast(I32))
+
+        nc.gpsimd.memset(key_scales[:].bitcast(I32), 0)
+        for q in range(4):
+            nc.gpsimd.dma_start(
+                key_scales[32 * q : 32 * q + 4, :].bitcast(I32).rearrange("r (z c) -> r z c", z=PASSES),
+                ky_scales[:, 4 * q : 4 * q + 4, :].rearrange("z r c -> r z c").bitcast(I32),
+            )
+
+        ident = keep.tile([P, P], F32, name="ident")
+        make_identity(nc, ident[:])
+        bias_ps = psum.tile([P, 2, P], F32, name="bias_ps")
+        for c in range(2):
+            nc.tensor.transpose(bias_ps[:, c, :], bi_col[:, c : c + 1].to_broadcast([P, P]), ident[:])
+        bias = keep.tile([P, I], F32, name="bias")
+        nc.scalar.copy(bias[:].rearrange("q (p c) -> q p c", c=2), bias_ps[:].rearrange("q c p -> q p c"))
+
+        acc = [psum.tile([P, I], F32, name=f"acc_{h}") for h in range(HALVES)]
+        picked = [[None] * PACK for z in range(PASSES)]
+        for z in range(PASSES):
+            for t in range(PACK):
+                picked[z][t] = keep.tile([P, J], F32, name=f"picked_{z}_{t}")
+                nc.scalar.activation(picked[z][t][:], xb_sb[z][:, t * S : (t + 1) * S].indirect(ent_list[:]), ACT.Copy)
+
+        u = [[keep.tile([P, P, PACK], BF16, name=f"u_{z}_{h}", align_bytes=64) for h in range(HALVES)] for z in range(PASSES)]
+        prod = [keep.tile([P, PACK, J], F32, name=f"prod_{z}") for z in range(PASSES)]
+
+        def gather_times(z, t):
+            nc.vector.tensor_tensor(prod[z][:, t, :], xf_sb[z][t][:].indirect(tok_list[:]), picked[z][t][:], ALU.mult)
+
+        def round_planes(z, h, planes):
+            nc.vector.tensor_tensor(
+                u[z][h][:, :, 0:planes],
+                prod[z][:, 0:planes, h * P : (h + 1) * P].rearrange("p t j -> p j t"),
+                fk_sb[:, z, 0:planes].unsqueeze(1).to_broadcast([P, P, planes]),
+                ALU.mult,
+            )
+
+        def round_plane(z, h, t, src):
+            nc.scalar.activation(u[z][h][:, :, t], src, ACT.Copy, scale=fk_sb[:, z, t : t + 1])
+
+        def multiply(z, h):
+            words = keep.tile([P, P], U32, name=f"u_words_{z}_{h}", align_bytes=64)
+            scales = keep.tile([P, P], U8, name=f"u_scales_{z}_{h}", align_bytes=64)
+            nc.vector.quantize_mx(
+                out=words[:].bitcast(E5M2X4), scales=scales[:], in_=u[z][h][:].rearrange("p j t -> p (j t)")
+            )
+            nc.tensor.matmul_mx(
+                out=acc[h][:],
+                lhsT=words[:].bitcast(E5M2X4),
+                lhsT_scale=scales[:],
+                rhs=key_words[:, z, :].bitcast(E5M2X4),
+                rhs_scale=key_scales[:, z * I : (z + 1) * I],
+                start=(z == 0),
+                stop=(z == PASSES - 1),
+            )
+
+        for t in range(PACK):
+            gather_times(0, t)
+        for h in range(HALVES):
+            round_planes(0, h, PACK)
+        last = PACK - 1
+        gather_times(1, 0)
+        for h in range(HALVES):
+            multiply(0, h)
+        round_plane(1, 0, 0, prod[1][:, 0, 0:P])
+        for t in range(1, last):
+            gather_times(1, t)
+            round_plane(1, 0, t, prod[1][:, t, 0:P])
+        round_planes(1, 1, last)
+
+        tail = keep.tile([P, P], F32, name="tail")
+        nc.vector.tensor_tensor(
+            prod[1][:, last, 0:P], xf_sb[1][last][:].indirect(tok_list[:, 0:LIST_COLS]), picked[1][last][:, 0:P], ALU.mult
+        )
+        nc.scalar.activation(tail[:], xf_sb[1][last][:].indirect(tok_list[:, LIST_COLS : 2 * LIST_COLS]), ACT.Copy)
+        nc.vector.scalar_tensor_tensor(
+            u[1][1][:, :, last], tail[:], fk_sb[:, 1, last : last + 1], picked[1][last][:, P : 2 * P], ALU.mult, ALU.mult
+        )
+        round_plane(1, 0, last, prod[1][:, last, 0:P])
+        for h in range(HALVES):
+            multiply(1, h)
+
+        score = [keep.tile([P, I], F32, name=f"score_{h}") for h in range(HALVES)]
+        size = [keep.tile([P, I], F32, name=f"size_{h}") for h in range(HALVES)]
+        total = [keep.tile([P, I // BUNDLE], F32, name=f"total_{h}") for h in range(HALVES)]
+        centred = [keep.tile([P, I], F32, name=f"centred_{h}") for h in range(HALVES)]
+        result = [keep.tile([P, I], F32, name=f"result_{h}") for h in range(HALVES)]
+        for h in range(HALVES):
+            nc.vector.tensor_tensor(score[h][:], acc[h][:], bias[:], ALU.add)
+            nc.scalar.activation(size[h][:], score[h][:], ACT.Abs)
+        for h in range(HALVES):
+            nc.vector.tensor_reduce(
+                total[h][:], score[h][:].rearrange("p (g m) -> p g m", m=BUNDLE), mybir.AxisListType.X, ALU.add
+            )
+        for h in range(HALVES):
+            nc.vector.scalar_tensor_tensor(
+                centred[h][:].rearrange("p (g m) -> p g m", m=BUNDLE),
+                total[h][:].unsqueeze(2).to_broadcast([P, I // BUNDLE, BUNDLE]),
+                -1.0 / BUNDLE,
+                score[h][:].rearrange("p (g m) -> p g m", m=BUNDLE),
+                ALU.mult,
+                ALU.add,
+            )
+        for h in range(HALVES):
+            nc.vector.tensor_tensor(result[h][:], centred[h][:], size[h][:], ALU.mult)
+            nc.sync.dma_start(out[h * P : (h + 1) * P, :], result[h][:])

@@ -22,40 +22,49 @@ K_PASS = P * PACK
 PASSES = K // K_PASS
 HALVES = J // P
 LIST_COLS = P // 16
+ORDER = ((0, 1, 2, 3), (2, 0, 1, 3))
+PICK_ORDER = ((0, 1, 2, 3), (2, 3, 0, 1))
+Q = P // 2
 
 
 def tile_list_scores_products_given_centred_kernel(tc, xf, xb, fk, ky_words, ky_scales, bi, offs, offs2, out):
     nc = tc.nc
     with ExitStack() as ctx:
         keep = ctx.enter_context(tc.tile_pool(name="keep", bufs=1))
+        ring = ctx.enter_context(tc.tile_pool(name="ring", bufs=2))
         psum = ctx.enter_context(tc.psum_pool(name="psum", bufs=1))
 
         tok_list = keep.tile([P, J // 16], U16, name="tok_list")
         ent_list = keep.tile([P, J // 16], U16, name="ent_list")
-        xb_sb = [keep.tile([P, PACK * S], F32, name=f"xb_{z}") for z in range(PASSES)]
+        xb_sb = [[keep.tile([P, 2 * S], F32, name=f"xb_{z}_{w}") for w in range(2)] for z in range(PASSES)]
         xf_sb = [[keep.tile([P, T], F32, name=f"xf_{z}_{t}") for t in range(PACK)] for z in range(PASSES)]
         fk_sb = keep.tile([P, PASSES, 2 * PACK], F32, name="fk_sb")
         bi_col = keep.tile([P, 2], F32, name="bi_col")
         key_words = keep.tile([P, PASSES, I], U32, name="key_words", align_bytes=64)
         key_scales = keep.tile([P, PASSES * I], U8, name="key_scales", align_bytes=64)
 
-        def load_xb(z):
+        def load_xb(z, w):
             rows = xb[z * K_PASS : (z + 1) * K_PASS, :]
-            nc.sync.dma_start(xb_sb[z][:], rows.rearrange("(p t) s -> p (t s)", t=PACK))
+            nc.sync.dma_start(xb_sb[z][w][:], rows.rearrange("(p t) s -> p (t s)", t=PACK)[:, 2 * w * S : 2 * (w + 1) * S])
 
         def load_xf(z, t):
             rows = xf[z * K_PASS : (z + 1) * K_PASS, :]
             nc.sync.dma_start(xf_sb[z][t][:], rows.rearrange("(p t) c -> p t c", t=PACK)[:, t, :])
 
-        load_xb(0)
+        load_xb(0, 0)
         nc.sync.dma_start(ent_list[:], offs2)
-        nc.sync.dma_start(tok_list[:], offs)
-        load_xb(1)
-        nc.sync.dma_start(bi_col[:], bi.rearrange("o (p c) -> p (o c)", c=2))
         nc.sync.dma_start(fk_sb[:, :, 0:PACK], fk.rearrange("(z p t) o -> p z (t o)", z=PASSES, t=PACK))
-        for z in range(PASSES):
-            for t in range(PACK):
-                load_xf(z, t)
+        load_xb(0, 1)
+        nc.sync.dma_start(tok_list[:], offs)
+        load_xf(0, 0)
+        load_xf(0, 1)
+        load_xb(1, 1)
+        nc.sync.dma_start(bi_col[:], bi.rearrange("o (p c) -> p (o c)", c=2))
+        load_xf(0, 2)
+        load_xf(0, 3)
+        load_xb(1, 0)
+        for t in ORDER[1]:
+            load_xf(1, t)
         nc.sync.dma_start(key_words[:].bitcast(I32), ky_words.rearrange("z p c r -> p z (c r)").bitcast(I32))
 
         nc.gpsimd.memset(key_scales[:].bitcast(I32), 0)
@@ -74,34 +83,28 @@ def tile_list_scores_products_given_centred_kernel(tc, xf, xb, fk, ky_words, ky_
         nc.scalar.copy(bias[:].rearrange("q (p c) -> q p c", c=2), bias_ps[:].rearrange("q c p -> q p c"))
 
         acc = [psum.tile([P, I], F32, name=f"acc_{h}") for h in range(HALVES)]
-        picked = [[None] * PACK for z in range(PASSES)]
+        scaled = [[None] * PACK for z in range(PASSES)]
         for z in range(PASSES):
-            for t in range(PACK):
-                picked[z][t] = keep.tile([P, J], F32, name=f"picked_{z}_{t}")
-                nc.scalar.activation(picked[z][t][:], xb_sb[z][:, t * S : (t + 1) * S].indirect(ent_list[:]), ACT.Copy)
+            for t in PICK_ORDER[z]:
+                picked = ring.tile([P, J], F32, name="picked")
+                nc.scalar.activation(picked[:], xb_sb[z][t // 2][:, (t % 2) * S : (t % 2 + 1) * S].indirect(ent_list[:]), ACT.Copy)
+                scaled[z][t] = keep.tile([P, J], F32, name=f"scaled_{z}_{t}")
+                nc.scalar.activation(scaled[z][t][:], picked[:], ACT.Copy, scale=fk_sb[:, z, t : t + 1])
 
-        u = [[keep.tile([P, P, PACK], BF16, name=f"u_{z}_{h}", align_bytes=64) for h in range(HALVES)] for z in range(PASSES)]
+        u = [keep.tile([P, J, PACK], BF16, name=f"u_{z}", align_bytes=64) for z in range(PASSES)]
         prod = [keep.tile([P, PACK, J], F32, name=f"prod_{z}") for z in range(PASSES)]
 
         def gather_times(z, t):
-            nc.vector.tensor_tensor(prod[z][:, t, :], xf_sb[z][t][:].indirect(tok_list[:]), picked[z][t][:], ALU.mult)
+            nc.vector.tensor_tensor(prod[z][:, t, :], xf_sb[z][t][:].indirect(tok_list[:]), scaled[z][t][:], ALU.mult)
 
-        def round_planes(z, h, planes):
-            nc.vector.tensor_tensor(
-                u[z][h][:, :, 0:planes],
-                prod[z][:, 0:planes, h * P : (h + 1) * P].rearrange("p t j -> p j t"),
-                fk_sb[:, z, 0:planes].unsqueeze(1).to_broadcast([P, P, planes]),
-                ALU.mult,
-            )
-
-        def round_plane(z, h, t, src):
-            nc.scalar.activation(u[z][h][:, :, t], src, ACT.Copy, scale=fk_sb[:, z, t : t + 1])
+        def round_planes(z, planes):
+            nc.vector.tensor_copy(u[z][:, :, 0:planes], prod[z][:, 0:planes, :].rearrange("p t j -> p j t"))
 
         def multiply(z, h):
             words = keep.tile([P, P], U32, name=f"u_words_{z}_{h}", align_bytes=64)
             scales = keep.tile([P, P], U8, name=f"u_scales_{z}_{h}", align_bytes=64)
             nc.vector.quantize_mx(
-                out=words[:].bitcast(E5M2X4), scales=scales[:], in_=u[z][h][:].rearrange("p j t -> p (j t)")
+                out=words[:].bitcast(E5M2X4), scales=scales[:], in_=u[z][:, h * P : (h + 1) * P, :].rearrange("p j t -> p (j t)")
             )
             nc.tensor.matmul_mx(
                 out=acc[h][:],
@@ -115,27 +118,37 @@ def tile_list_scores_products_given_centred_kernel(tc, xf, xb, fk, ky_words, ky_
 
         for t in range(PACK):
             gather_times(0, t)
-        for h in range(HALVES):
-            round_planes(0, h, PACK)
-        last = PACK - 1
-        gather_times(1, 0)
+        round_planes(0, PACK)
+        gather_times(1, 2)
         for h in range(HALVES):
             multiply(0, h)
-        round_plane(1, 0, 0, prod[1][:, 0, 0:P])
-        for t in range(1, last):
-            gather_times(1, t)
-            round_plane(1, 0, t, prod[1][:, t, 0:P])
-        round_planes(1, 1, last)
+        u_q = u[1][:].rearrange("p (h e j) t -> p h e j t", h=HALVES, e=2)
+        prod_q = prod[1][:].rearrange("p t (h e j) -> p t h e j", h=HALVES, e=2)
+        nc.scalar.activation(u_q[:, :, 0, :, 2], prod_q[:, 2, :, 0, :], ACT.Copy)
+        nc.vector.tensor_copy(u_q[:, :, 1, :, 2], prod_q[:, 2, :, 1, :])
+        gather_times(1, 0)
+        gather_times(1, 1)
+        round_planes(1, 2)
 
-        tail = keep.tile([P, P], F32, name="tail")
-        nc.vector.tensor_tensor(
-            prod[1][:, last, 0:P], xf_sb[1][last][:].indirect(tok_list[:, 0:LIST_COLS]), picked[1][last][:, 0:P], ALU.mult
-        )
-        nc.scalar.activation(tail[:], xf_sb[1][last][:].indirect(tok_list[:, LIST_COLS : 2 * LIST_COLS]), ACT.Copy)
-        nc.vector.scalar_tensor_tensor(
-            u[1][1][:, :, last], tail[:], fk_sb[:, 1, last : last + 1], picked[1][last][:, P : 2 * P], ALU.mult, ALU.mult
-        )
-        round_plane(1, 0, last, prod[1][:, last, 0:P])
+        last = PACK - 1
+        tail = [keep.tile([P, Q], F32, name=f"tail_{h}") for h in range(HALVES)]
+        for h in range(HALVES):
+            first = slice(h * P, h * P + Q)
+            nc.vector.tensor_tensor(
+                prod[1][:, last, first],
+                xf_sb[1][last][:].indirect(tok_list[:, first.start // 16 : first.stop // 16]),
+                scaled[1][last][:, first],
+                ALU.mult,
+            )
+            second = slice(h * P + Q, (h + 1) * P)
+            nc.scalar.activation(
+                tail[h][:], xf_sb[1][last][:].indirect(tok_list[:, second.start // 16 : second.stop // 16]), ACT.Copy
+            )
+        for h in range(HALVES):
+            first = slice(h * P, h * P + Q)
+            second = slice(h * P + Q, (h + 1) * P)
+            nc.vector.tensor_tensor(u[1][:, second, last], tail[h][:], scaled[1][last][:, second], ALU.mult)
+            nc.scalar.activation(u[1][:, first, last], prod[1][:, last, first], ACT.Copy)
         for h in range(HALVES):
             multiply(1, h)
 

@@ -43,30 +43,31 @@ def tile_list_scores_products_given_centred_kernel(tc, xf, xb, fk, ky_words, ky_
         key_words = keep.tile([P, PASSES, I], U32, name="key_words", align_bytes=64)
         key_scales = keep.tile([P, PASSES * I], U8, name="key_scales", align_bytes=64)
 
-        def load_xb(z, w):
+        def load_xb(queue, z, w):
             rows = xb[z * K_PASS : (z + 1) * K_PASS, :]
-            nc.sync.dma_start(xb_sb[z][w][:], rows.rearrange("(p t) s -> p (t s)", t=PACK)[:, 2 * w * S : 2 * (w + 1) * S])
+            queue.dma_start(xb_sb[z][w][:], rows.rearrange("(p t) s -> p (t s)", t=PACK)[:, 2 * w * S : 2 * (w + 1) * S])
 
         def load_xf(z, t):
             rows = xf[z * K_PASS : (z + 1) * K_PASS, :]
             nc.sync.dma_start(xf_sb[z][t][:], rows.rearrange("(p t) c -> p t c", t=PACK)[:, t, :])
 
-        load_xb(0, 0)
-        nc.sync.dma_start(ent_list[:], offs2)
-        nc.sync.dma_start(fk_sb[:, :, 0:PACK], fk.rearrange("(z p t) o -> p z (t o)", z=PASSES, t=PACK))
-        load_xb(0, 1)
-        nc.sync.dma_start(tok_list[:], offs)
+        nc.scalar.dma_start(bi_col[:], bi.rearrange("o (p c) -> p (o c)", c=2))
+        load_xb(nc.scalar, 0, 0)
+        nc.scalar.dma_start(fk_sb[:, :, 0:PACK], fk.rearrange("(z p t) o -> p z (t o)", z=PASSES, t=PACK))
+        load_xb(nc.scalar, 0, 1)
+        load_xb(nc.scalar, 1, 1)
         load_xf(0, 0)
-        load_xf(0, 1)
-        load_xb(1, 1)
-        nc.sync.dma_start(bi_col[:], bi.rearrange("o (p c) -> p (o c)", c=2))
-        load_xf(0, 2)
-        load_xf(0, 3)
-        load_xb(1, 0)
+        nc.sync.dma_start(ent_list[:], offs2)
+        nc.sync.dma_start(tok_list[:], offs)
+        for t in range(1, PACK):
+            load_xf(0, t)
+        load_xb(nc.sync, 1, 0)
         for t in ORDER[1]:
             load_xf(1, t)
         nc.sync.dma_start(key_words[:].bitcast(I32), ky_words.rearrange("z p c r -> p z (c r)").bitcast(I32))
 
+        ident = keep.tile([P, P], F32, name="ident")
+        make_identity(nc, ident[:])
         nc.gpsimd.memset(key_scales[:].bitcast(I32), 0)
         for q in range(4):
             nc.gpsimd.dma_start(
@@ -74,13 +75,11 @@ def tile_list_scores_products_given_centred_kernel(tc, xf, xb, fk, ky_words, ky_
                 ky_scales[:, 4 * q : 4 * q + 4, :].rearrange("z r c -> r z c").bitcast(I32),
             )
 
-        ident = keep.tile([P, P], F32, name="ident")
-        make_identity(nc, ident[:])
         bias_ps = psum.tile([P, 2, P], F32, name="bias_ps")
         for c in range(2):
             nc.tensor.transpose(bias_ps[:, c, :], bi_col[:, c : c + 1].to_broadcast([P, P]), ident[:])
         bias = keep.tile([P, I], F32, name="bias")
-        nc.scalar.copy(bias[:].rearrange("q (p c) -> q p c", c=2), bias_ps[:].rearrange("q c p -> q p c"))
+        nc.scalar.activation(bias[:].rearrange("q (p c) -> q p c", c=2), bias_ps[:].rearrange("q c p -> q p c"), ACT.Copy)
 
         acc = [psum.tile([P, I], F32, name=f"acc_{h}") for h in range(HALVES)]
         scaled = [[None] * PACK for z in range(PASSES)]

from contextlib import ExitStack

import concourse.mybir as mybir
from concourse.masks import make_identity

K, T, J, I, S, BUNDLE = 1024, 1024, 256, 256, 512, 8
FLOPS = 2 * K * J * I

F32 = mybir.dt.float32
BF16 = mybir.dt.bfloat16
I32 = mybir.dt.int32
U32 = mybir.dt.uint32
U16 = mybir.dt.uint16
U8 = mybir.dt.uint8
E5M2X4 = mybir.dt.float8_e5m2_x4
ALU = mybir.AluOpType
ACT = mybir.ActivationFunctionType

P = 128
PACK = 4
K_PASS = P * PACK
PASSES = K // K_PASS
HALVES = J // P
LIST_COLS = P // 16
ORDER = ((0, 1, 2, 3), (2, 0, 1, 3))
PICK_ORDER = ((0, 1, 2, 3), (2, 3, 0, 1))
Q = P // 2


def tile_list_scores_products_given_centred_kernel(tc, xf, xb, fk, ky_words, ky_scales, bi, offs, offs2, out):
    nc = tc.nc
    with ExitStack() as ctx:
        keep = ctx.enter_context(tc.tile_pool(name="keep", bufs=1))
        ring = ctx.enter_context(tc.tile_pool(name="ring", bufs=2))
        psum = ctx.enter_context(tc.psum_pool(name="psum", bufs=1))

        tok_list = keep.tile([P, J // 16], U16, name="tok_list")
        ent_list = keep.tile([P, J // 16], U16, name="ent_list")
        xb_sb = [[keep.tile([P, 2 * S], F32, name=f"xb_{z}_{w}") for w in range(2)] for z in range(PASSES)]
        xf_sb = [[keep.tile([P, T], F32, name=f"xf_{z}_{t}") for t in range(PACK)] for z in range(PASSES)]
        fk_sb = keep.tile([P, PASSES, 2 * PACK], F32, name="fk_sb")
        bi_col = keep.tile([P, 2], F32, name="bi_col")
        key_words = keep.tile([P, PASSES, I], U32, name="key_words", align_bytes=64)
        key_scales = keep.tile([P, PASSES * I], U8, name="key_scales", align_bytes=64)

        def load_xb(queue, z, w):
            rows = xb[z * K_PASS : (z + 1) * K_PASS, :]
            queue.dma_start(xb_sb[z][w][:], rows.rearrange("(p t) s -> p (t s)", t=PACK)[:, 2 * w * S : 2 * (w + 1) * S])

        def load_xf(z, t):
            rows = xf[z * K_PASS : (z + 1) * K_PASS, :]
            nc.sync.dma_start(xf_sb[z][t][:], rows.rearrange("(p t) c -> p t c", t=PACK)[:, t, :])

        nc.scalar.dma_start(bi_col[:], bi.rearrange("o (p c) -> p (o c)", c=2))
        load_xb(nc.scalar, 0, 0)
        nc.scalar.dma_start(fk_sb[:, :, 0:PACK], fk.rearrange("(z p t) o -> p z (t o)", z=PASSES, t=PACK))
        load_xb(nc.scalar, 0, 1)
        load_xb(nc.scalar, 1, 1)
        load_xf(0, 0)
        nc.sync.dma_start(ent_list[:], offs2)
        nc.sync.dma_start(tok_list[:], offs)
        for t in range(1, PACK):
            load_xf(0, t)
        load_xb(nc.sync, 1, 0)
        for t in ORDER[1]:
            load_xf(1, t)
        nc.sync.dma_start(key_words[:].bitcast(I32), ky_words.rearrange("z p c r -> p z (c r)").bitcast(I32))

        ident = keep.tile([P, P], F32, name="ident")
        make_identity(nc, ident[:])
        nc.gpsimd.memset(key_scales[:].bitcast(I32), 0)
        for q in range(4):
            nc.gpsimd.dma_start(
                key_scales[32 * q : 32 * q + 4, :].bitcast(I32).rearrange("r (z c) -> r z c", z=PASSES),
                ky_scales[:, 4 * q : 4 * q + 4, :].rearrange("z r c -> r z c").bitcast(I32),
            )

        bias_ps = psum.tile([P, 2, P], F32, name="bias_ps")
        for c in range(2):
            nc.tensor.transpose(bias_ps[:, c, :], bi_col[:, c : c + 1].to_broadcast([P, P]), ident[:])
        bias = keep.tile([P, I], F32, name="bias")
        nc.scalar.activation(bias[:].rearrange("q (p c) -> q p c", c=2), bias_ps[:].rearrange("q c p -> q p c"), ACT.Copy)

        acc = [psum.tile([P, I], F32, name=f"acc_{h}") for h in range(HALVES)]
        scaled = [[None] * PACK for z in range(PASSES)]
        for z in range(PASSES):
            for t in PICK_ORDER[z]:
                picked = ring.tile([P, J], F32, name="picked")
                nc.scalar.activation(picked[:], xb_sb[z][t // 2][:, (t % 2) * S : (t % 2 + 1) * S].indirect(ent_list[:]), ACT.Copy)
                scaled[z][t] = keep.tile([P, J], F32, name=f"scaled_{z}_{t}")
                nc.scalar.activation(scaled[z][t][:], picked[:], ACT.Copy, scale=fk_sb[:, z, t : t + 1])

        u = [keep.tile([P, J, PACK], BF16, name=f"u_{z}", align_bytes=64) for z in range(PASSES)]
        prod = [keep.tile([P, PACK, J], F32, name=f"prod_{z}") for z in range(PASSES)]

        def gather_times(z, t):
            nc.vector.tensor_tensor(prod[z][:, t, :], xf_sb[z][t][:].indirect(tok_list[:]), scaled[z][t][:], ALU.mult)

        def round_planes(z, planes):
            nc.vector.tensor_copy(u[z][:, :, 0:planes], prod[z][:, 0:planes, :].rearrange("p t j -> p j t"))

        def multiply(z, h):
            words = keep.tile([P, P], U32, name=f"u_words_{z}_{h}", align_bytes=64)
            scales = keep.tile([P, P], U8, name=f"u_scales_{z}_{h}", align_bytes=64)
            nc.vector.quantize_mx(
                out=words[:].bitcast(E5M2X4), scales=scales[:], in_=u[z][:, h * P : (h + 1) * P, :].rearrange("p j t -> p (j t)")
            )
            nc.tensor.matmul_mx(
                out=acc[h][:],
                lhsT=words[:].bitcast(E5M2X4),
                lhsT_scale=scales[:],
                rhs=key_words[:, z, :].bitcast(E5M2X4),
                rhs_scale=key_scales[:, z * I : (z + 1) * I],
                start=(z == 0),
                stop=(z == PASSES - 1),
            )

        for t in range(PACK):
            gather_times(0, t)
        round_planes(0, PACK)
        gather_times(1, 2)
        for h in range(HALVES):
            multiply(0, h)
        u_q = u[1][:].rearrange("p (h e j) t -> p h e j t", h=HALVES, e=2)
        prod_q = prod[1][:].rearrange("p t (h e j) -> p t h e j", h=HALVES, e=2)
        nc.scalar.activation(u_q[:, :, 0, :, 2], prod_q[:, 2, :, 0, :], ACT.Copy)
        nc.vector.tensor_copy(u_q[:, :, 1, :, 2], prod_q[:, 2, :, 1, :])
        gather_times(1, 0)
        gather_times(1, 1)
        round_planes(1, 2)

        last = PACK - 1
        tail = [keep.tile([P, Q], F32, name=f"tail_{h}") for h in range(HALVES)]
        for h in range(HALVES):
            first = slice(h * P, h * P + Q)
            nc.vector.tensor_tensor(
                prod[1][:, last, first],
                xf_sb[1][last][:].indirect(tok_list[:, first.start // 16 : first.stop // 16]),
                scaled[1][last][:, first],
                ALU.mult,
            )
            second = slice(h * P + Q, (h + 1) * P)
            nc.scalar.activation(
                tail[h][:], xf_sb[1][last][:].indirect(tok_list[:, second.start // 16 : second.stop // 16]), ACT.Copy
            )
        for h in range(HALVES):
            first = slice(h * P, h * P + Q)
            second = slice(h * P + Q, (h + 1) * P)
            nc.vector.tensor_tensor(u[1][:, second, last], tail[h][:], scaled[1][last][:, second], ALU.mult)
            nc.scalar.activation(u[1][:, first, last], prod[1][:, last, first], ACT.Copy)
        for h in range(HALVES):
            multiply(1, h)

        score = [keep.tile([P, I], F32, name=f"score_{h}") for h in range(HALVES)]
        size = [keep.tile([P, I], F32, name=f"size_{h}") for h in range(HALVES)]
        total = [keep.tile([P, I // BUNDLE], F32, name=f"total_{h}") for h in range(HALVES)]
        centred = [keep.tile([P, I], F32, name=f"centred_{h}") for h in range(HALVES)]
        result = [keep.tile([P, I], F32, name=f"result_{h}") for h in range(HALVES)]
        for h in range(HALVES):
            nc.vector.tensor_tensor(score[h][:], acc[h][:], bias[:], ALU.add)
            nc.scalar.activation(size[h][:], score[h][:], ACT.Abs)
        for h in range(HALVES):
            nc.vector.tensor_reduce(
                total[h][:], score[h][:].rearrange("p (g m) -> p g m", m=BUNDLE), mybir.AxisListType.X, ALU.add
            )
        for h in range(HALVES):
            nc.vector.scalar_tensor_tensor(
                centred[h][:].rearrange("p (g m) -> p g m", m=BUNDLE),
                total[h][:].unsqueeze(2).to_broadcast([P, I // BUNDLE, BUNDLE]),
                -1.0 / BUNDLE,
                score[h][:].rearrange("p (g m) -> p g m", m=BUNDLE),
                ALU.mult,
                ALU.add,
            )
        for h in range(HALVES):
            nc.vector.tensor_tensor(result[h][:], centred[h][:], size[h][:], ALU.mult)
            nc.sync.dma_start(out[h * P : (h + 1) * P, :], result[h][:])
